import numpy as np, ml_dtypes
CORES = [2,6,10,14,18,22,26,30]
N = 8
import mx_ref
BF = ml_dtypes.bfloat16
def gentries(a):
    return np.ascontiguousarray(a.reshape(8, 16, -1).transpose(0, 2, 1)).reshape(8, -1)
def gtable(e):
    e = np.asarray(e); return np.ascontiguousarray(e.reshape(8, -1, 16).transpose(0, 2, 1)).reshape(128, -1).astype(np.int32)
def gcols(t, e):
    v = np.concatenate([t.reshape(8, 16, -1, 4), np.zeros((8, 16, 1, 4), BF)], axis=2)
    return np.ascontiguousarray(np.stack([v[g][:, e[g]] for g in range(8)])).reshape(128, -1)
def tile(rs):
    return np.stack(rs, axis=2).reshape(128, -1).astype(BF)
def pick(q, e):
    c = np.concatenate([q[0].reshape(128, -1, 4), np.zeros((128, 1, 4), np.uint8)], axis=1); s = np.concatenate([q[1], np.ones((16, 1), np.uint8)], axis=1)
    return (np.ascontiguousarray(c[:, e].reshape(128, -1)), np.ascontiguousarray(s[:, e]))
def join(*qs):
    return (np.concatenate([q[0] for q in qs], axis=1), np.concatenate([q[1] for q in qs], axis=1))
def put(q, e, v):
    c, s = q[0].reshape(128, -1, 4).copy(), q[1].copy(); c[:, e] = v[0].reshape(128, -1, 4); s[:, e] = v[1]
    return (c.reshape(128, -1), s)
def pk(c, s):
    return (np.ascontiguousarray(c), mx_ref.live(s))
def emit(q):
    return q[0], q[1]
def packed(v, rng):
    q = [mx_ref.quantize(np.ascontiguousarray(v[r])) for r in range(N)]
    return np.stack([a for a, b in q]), np.stack([mx_ref.plane(b, rng) for a, b in q])
def values_of_codes():
    e, c = np.zeros((128, 128, 4), np.float32), np.zeros((128, 2, 4), np.uint8)
    e[np.arange(128), np.arange(128), 0] = 1
    c[:127, :, 0] = np.arange(256).reshape(2, 128).T[:127]
    return mx_ref.matmul(mx_ref.quantize(e.reshape(128, 512).astype(BF)), (c.reshape(128, 8), np.full((16, 2), 127, np.uint8))).T.reshape(-1).astype(np.float64)
CODE_VALUE, SCALE_VALUE = values_of_codes(), 2.0 ** (np.arange(256) - 127.0)
def decode(q):
    return (CODE_VALUE[q[0]].reshape(16, 8, -1, 4) * SCALE_VALUE[q[1]][:, None, :, None] + 0.0).reshape(128, -1).astype(np.float32)
def f(rng, *shape):
    return mx_ref.flush((rng.standard_normal(shape, dtype=np.float32) * np.exp2(rng.integers(-2, 3, shape[:-1] + (1,)))).astype(BF))
def wide(rng, *shape, cols=0):
    v = rng.standard_normal(shape, dtype=np.float32) * np.exp2(rng.integers(-12, 13, shape)).astype(np.float32)
    if cols: v *= np.repeat(np.exp2(rng.integers(-cols, cols + 1, shape[:-2] + (1, shape[-1] // 4))) * (rng.random(shape[:-2] + (1, shape[-1] // 4)) > 0.0625), 4, axis=-1).astype(np.float32)
    return mx_ref.flush(v.astype(BF))
C = 384
MASK = [1, 2, 4]
ALIKE = 2
def numbers_of(rng):
    return {"x": np.array(f(rng, N, 128, 4 * C)), "u": np.array(f(rng, N, 128, 512)), "v": np.array(f(rng, N, 128, 512))}
def stored(k):
    return {"se": np.stack([gtable(k[r].reshape(8, 2 * C)) for r in range(N)])}
def lists(rng):
    return stored(rng.permuted(np.tile(np.arange(C), (N, 8, 2, 1)), axis=3))
def layers(rng):
    return np.array(f(rng, N, 128, 2048)).reshape(N, 8, 16, 4, 8, 16, 4)
def weights(rng, w):
    c, s = packed(np.ascontiguousarray(w).reshape(N, 128, 2048), rng)
    return {"wc": c, "ws": s}
def setup_inputs(rng):
    return {**numbers_of(rng), **lists(rng), **weights(rng, layers(rng))}
def setup_inputs_ties(rng):
    d = numbers_of(rng)
    o = rng.permutation(N)
    k = rng.integers(-1, 2, (N, 8, 7, C)).astype(np.float32)
    k[o[1]] = 1
    x = d["x"].reshape(N, 8, 16, C, 4)
    x[:, :, :7, :, 0] = k.astype(BF)
    x[:, :, 8:] = 0
    a = np.exp2(rng.integers(-3, 4, (8, 1)).astype(np.float32))
    x[:, :, 8, :, 0] = (-3.0 * a).astype(BF)
    x[:, :, 10, :, 0] = (-0.0625 * a).astype(BF)
    x[:, :, 11, :, 0] = (0.28125 * a).astype(BF)
    c = np.ones(N, np.float32)
    c[o[0]] = 0
    c[o[2]] = -1
    u = d["u"].reshape(N, 128, 128, 4)
    for l in range(7):
        u[:, :, l::16] = 0
        for h in range(0, 128, 16): u[:, h + l, h + l, 0] = c.astype(BF)
    w = layers(rng)
    w[:, :, :, 0, :, :7] = 0
    w[:, :, :, :, :, 8:] = 0
    for g in range(8):
        w[:, g, 11, 0, g, 8, 0] = 112.0
        for b in range(4): w[:, g, 10, b, g, 9, 0] = -(1.125 + 0.25 * b) * 2.0 ** -5
    return {"x": x.reshape(N, 128, 4 * C), "u": u.reshape(N, 128, 512), "v": d["v"], **lists(rng), **weights(rng, w)}
def setup_inputs_near(rng):
    d = numbers_of(rng)
    k = np.where(((np.arange(N) & ALIKE) > 0) ^ (rng.random() < 0.5), 2.0 ** -30, 1.0)
    x = np.zeros((N, 8, 16, C, 4))
    s = rng.integers(-1, 2, (N, 8, 7, C)) * k[:, None, None, None]
    x[:, :, :7, :, 0] = 1.125 * s
    x[:, :, 8:15, :, 0] = -1.25 * s
    x[:, :, 15] = rng.choice([-1.0, 1.0], (N, 8, C, 4)) * (1.0 + 0.125 * rng.integers(0, 8, (N, 8, C, 4)) * (np.arange(4) > 1)) * 2.0 ** -30
    x[:, :, 15, :, 1] = 2.0 ** -30
    x[:, :, 7, :, 0] = 2.0 ** -30
    for r in range(N):
        at = [0, C - 1, int(rng.integers(C)), int(rng.integers(C))]
        for g, j in zip(rng.permutation(8)[:4], at): x[r, g, int(rng.integers(7)), j, 0] = 2.0 ** 30 * rng.choice([-1.0, 1.0])
    u = d["u"].reshape(N, 128, 128, 4)
    w = np.zeros((N, 8, 16, 4, 8, 16, 4), np.float32)
    for g in range(8):
        w[:, g, 15, 1, g, 7, 0] = 32.0
        w[:, g, 15, 1, g, 15, 1] = 32.0
        w[:, g, 15, 2:, g, 15, 2:] = rng.choice([-1.0, 1.0], (N, 2, 2)) * (8.0 + rng.integers(0, 8, (N, 2, 2)))
    for l in range(7):
        u[:, :, l::16] = 0
        for g in range(8):
            h = 16 * g
            u[:, h + l, h + l, 0] = (1.125 * k).astype(np.float32).astype(BF)
            u[:, h + 8 + l, h + l, 0] = k.astype(np.float32).astype(BF)
            w[:, g, 15, 0, g, l, 0] = rng.choice([-1.0, 1.0], N) * 2.0 ** -8
    return {"x": x.astype(np.float32).reshape(N, 128, 4 * C).astype(BF), "u": u.reshape(N, 128, 512), "v": d["v"], **lists(rng), **weights(rng, w.astype(BF))}
def setup_inputs_odd(rng):
    d = numbers_of(rng)
    x = (1.0 + (2 * rng.integers(0, 64, (N, 8, 16, C, 4)) + 1) * 2.0 ** -7) * np.exp2(-rng.integers(0, 7, (N, 8, 16, C, 4)).astype(np.float64)) * rng.choice([-1.0, 1.0], (N, 8, 16, C, 4))
    n = 2 * rng.integers(4, 8, (N, 8, 7, C)) + 1
    c = rng.choice([-1.0, 1.0], (N, 8, 7, C)) * 2.0 ** -8
    x[:, :, 0, :, 0] = 1.96875 * 2.0 ** 8 * rng.choice([-1.0, 1.0], (N, 8, 1))
    x[:, :, 1:8, :, 0] = c * n
    x[:, :, 8:15, :, 0] = -8.0 * c
    x[:, :, 8:15, :, 1] = -c * (n - 8 + rng.choice([-0.5, 0.5], (N, 8, 7, C)))
    u = d["u"].reshape(N, 128, 128, 4)
    for l in range(7):
        u[:, :, l::16] = 0
        for h in range(0, 128, 16):
            u[:, h + 1 + l, h + l, 0] = 1.0
            u[:, h + 8 + l, h + l, :2] = 1.0
    w = layers(rng)
    w[:, :, :, 0, :, :15] = 0
    w[:, :, :, 1, :, 8:15] = 0
    w[:, :, 0, :, :, :, 0] = 0
    return {"x": x.astype(np.float32).reshape(N, 128, 4 * C).astype(BF), "u": u.reshape(N, 128, 512), "v": d["v"], **lists(rng), **weights(rng, w)}
def setup_inputs_ends(rng):
    d = numbers_of(rng)
    o = rng.permutation(N) % 4
    j = np.arange(C)
    s = rng.choice([-1.0, 1.0], (N, 128, C, 4))
    s[o == 0] = -1
    s[o == 1] = (1.0 - j % 2 * 2.0)[:, None]
    x = s * (0.83 + 0.02 * rng.random((N, 128, C, 4))) * 2.0 ** 30
    x[o == 3] = -(1.0 + 0.125 * rng.integers(0, 8, (N, 128, C, 4))[o == 3]) * 2.0 ** -30
    size = np.where(o == 3, 2.0 ** -30, 2.0 ** 30)
    a = rng.permuted(np.tile(np.arange(8) % 2 * 2.0 - 1.0, (N, 7, 1)), axis=2).transpose(0, 2, 1) * size[:, None, None]
    for r in range(N): a[r, rng.permutation(8)[:2]] = 0
    u = d["u"].reshape(N, 128, 8, 16, 4)
    u[:, :, :, :7] = a.astype(np.float32).astype(BF)[:, None, :, :, None]
    v = rng.choice([-1.0, 1.0], (N, 128, 512)) * np.where(o % 2 == 0, 2.0 ** 30, 2.0 ** -30)[:, None, None]
    t = np.stack([j, (j + 2) % C, C - 1 - j, (j + 1) % C])
    k = rng.integers(0, 2, (N, 8, 2)) + 2 * (rng.permutation(8) < 4)[:, None]
    w = np.zeros((N, 128, 4, 128, 4), np.float32)
    i = np.arange(128)
    for b in range(4): w[:, i, b, i, b] = np.where(o == 3, 32.0, -1.0)[:, None]
    return {"x": x.astype(np.float32).reshape(N, 128, 4 * C).astype(BF), "u": u.reshape(N, 128, 512), "v": v.astype(np.float32).astype(BF), **stored(t[k]), **weights(rng, w.astype(BF))}
def setup_inputs_spread(rng):
    d = setup_inputs(rng)
    d["x"] = wide(rng, N, 128, 4 * C, cols=6)
    return d
def check_inputs(d):
    b = []
    for k in ("x", "u", "v"):
        a = np.abs(d[k].astype(np.float32))
        if not (np.isfinite(a).all() and ((a == 0) | (a >= 2.0 ** -30) & (a <= 2.0 ** 30)).all()): b.append("a value of " + k)
    none, least, most = [emit(mx_ref.quantize(np.full((128, 16), k, np.float32).astype(BF)))[1][0, 0] for k in (0.0, 2.0 ** -8, 2.0 ** 8)]
    for r in range(N):
        if not (np.sort(gentries(d["se"][r]).reshape(8, 2, C), axis=2) == np.arange(C)).all(): b.append("se: a list that is no permutation")
        if ((d["wc"][r] == 0x7F) | (d["wc"][r] == 0xFF)).any(): b.append("wc: a code that is no number")
        s = mx_ref.live(d["ws"][r])
        if ((s != none) & ((s < least) | (s > most))).any(): b.append("ws: a scale out of range")
    return b
def reference(x, u, v, se, wc, ws):
    qu = [mx_ref.quantize(u[r]) for r in range(N)]
    lay = [pk(wc[r], ws[r]) for r in range(N)]
    sec = [gentries(se[r]).reshape(8, 2, C) for r in range(N)]
    now = [x[r] for r in range(N)]
    g = np.arange(8)[:, None]
    for m in MASK:
        new, out = [], []
        for r in range(N):
            p = r ^ m
            bit = (mx_ref.matmul(qu[r], mx_ref.quantize(now[r])).reshape(8, 16, C)[:, :7] > 0).astype(np.int64)
            i = np.tile(np.arange(C), (8, 1))
            k = i
            for l in range(6):
                b = bit[g, l, i]
                i, k = sec[r][g, b, i], sec[p][g, 1 - b, k]
            end = bit[g, 6, k]
            turn = np.arange(C) ^ end ^ end[:, np.arange(C) ^ 1]
            new.append(np.stack([sec[p][g, 1 - b, turn[g, sec[r][:, b]]] for b in range(2)], axis=1))
            z = mx_ref.quantize(((gcols(now[r], i).astype(np.float32) + gcols(now[r], k).astype(np.float32)) * np.float32(0.5)).astype(BF))
            out.append(mx_ref.quantize(tile([mx_ref.matmul(pick(lay[r], np.arange(128 * b, 128 * b + 128)), z) * np.float32(0.03125) for b in range(4)])))
        now = [(now[r].astype(np.float32) + gcols(decode(out[r ^ m]).astype(BF), new[r][:, 0]).astype(np.float32)).astype(BF) for r in range(N)]
        sec = new
    y, so = np.zeros((N, 128, C), np.float32), np.zeros((N, 8, 2 * C), np.float32)
    oc, osc = np.zeros((N, 128, 4 * C), np.uint8), np.zeros((N, 16, C), np.uint8)
    for r in range(N):
        q = mx_ref.quantize(now[r])
        y[r] = mx_ref.matmul(mx_ref.quantize(v[r]), q)
        so[r] = sec[r].reshape(8, 2 * C)
        oc[r], osc[r] = emit(q)
    return {"y": y, "so": so, "oc": oc, "osc": osc}

@@ -1,0 +1,377 @@
+from concourse.mybir import dt, AluOpType, ActivationFunctionType
+
+C = 384
+NB = C // 16
+MASK = [1, 2, 4]
+CH = [(0, 256), (256, 384)]
+Q = 2.0 ** -13
+SCRATCH, SEMAPHORES = {}, ["v", "s", "t", "i", "loc"]
+
+
+def _sb(names, n, dtype, *more):
+    for k in names.split(): SCRATCH[k] = ("sbuf", [128, n] + list(more), dtype)
+
+
+def _codes(names, n):
+    for k in names.split():
+        _sb(k + "q", n, "float8_e4m3fn_x4")
+        _sb(k + "s", n, "uint8")
+
+
+_sb("ua ub vt et0 et1 et2 et3 one", 512, "bfloat16")
+_codes("pa pb p6 pv e0 e1 e2 e3", 128)
+_codes("lay", 512)
+_sb("x0 x1 x2 x3 xh xi zt ht dd t2", 4 * C, "bfloat16")
+_codes("x z h0 h1 h2 l0 l1 l2", C)
+_sb("ll0 ll1 ll2 ls0 ls1 ls2 ls3", 48, "uint16")
+SCRATCH["ps"] = ("psum", [128, 4096], "float32")
+_sb("bt tr", NB, "bfloat16", 32)
+_sb("idc mk mk4 mkc r4 km ks e6", C, "bfloat16")
+_sb("r16 sp yy tm tn", 768, "bfloat16")
+_sb("sw rw5 rw4 rw3 sod", 768, "float32")
+_sb("rw2 a1 am an yd", C, "float32")
+_sb("ia ib", C, "int32")
+_sb("sei", 48, "int32")
+_sb("ip iq ya yb yi yw", 24, "int32")
+_sb("i8", 8, "int32")
+_sb("ci cb hb fk k2 w4 fe sm df", 24, "float32")
+_sb("pq pd", 2, "float32")
+_sb("ci2 e15", NB, "float32", 2)
+_sb("dl mm fm", NB, "float32", 5)
+_sb("o0 o1 o2 o3 o4 o5 oa oi ob oc6 oe ot", 24, "uint16")
+_sb("oi6 oz od", 96, "uint16")
+_sb("o6", 8, "uint16")
+SEMAPHORES += ["d%d" % k for k in range(20)]
+SEMAPHORES += ["h%d_%d" % (r, c) for r in range(3) for c in range(2)] + ["n%d" % r for r in range(3)]
+
+
+def rank_program(g, core, T, topo):
+    rank = T.rank_of(core)
+    if rank is None:
+        return
+    A, F = AluOpType, ActivationFunctionType
+    queue = {"v": g.vector, "s": g.scalar, "t": g.tensor, "g": g, "y": g.sync}
+    count = {"v": 0, "s": 0, "t": 0, "i": 0, "d": 0, "loc": 0}
+    waited, writer, readers = {}, {}, {}
+
+    def wait(q, s, n):
+        if waited.get((q, s), 0) < n:
+            queue[q].wait_ge(T.sem[s], n)
+            waited[(q, s)] = n
+
+    def before(q, R, W):
+        need = {}
+        for k in R:
+            if k in writer: need[writer[k][1]] = max(need.get(writer[k][1], 0), writer[k][2])
+        for k in W:
+            for o in ([writer[k]] if k in writer else []) + readers.get(k, []):
+                if o[0] != q: need[o[1]] = max(need.get(o[1], 0), o[2])
+        for s in need: wait(q, s, need[s])
+
+    def after(q, s, n, R, W):
+        for k in W: writer[k], readers[k] = (q, s, n), []
+        for k in R: readers.setdefault(k, []).append((q, s, n))
+
+    def op(q, call, R, W, *a, **kw):
+        R, W = R.split(), W.split()
+        before(q, R, W)
+        s = "i" if q == "g" else q
+        call(*a, **kw).then_inc(T.sem[s], 1)
+        count[s] += 1
+        after(q, s, count[s], R, W)
+
+    def V(call, R, W, *a): op("v", call, R, W, *a)
+
+    def S(R, W, out, in_, func=F.Copy, **kw): op("s", g.scalar.activation, R, W, out, in_, func, **kw)
+
+    def D(q, R, W, out, in_):
+        R, W = R.split(), W.split()
+        before(q, R, W)
+        s = "d%d" % count["d"]
+        count["d"] += 1
+        queue[q].dma_start(out, in_).then_inc(T.sem[s], 16)
+        after("dma", s, 16, R, W)
+        return s
+
+    def send(dst, R, sem, pairs):
+        rid, pid, _ = topo.addr(dst)
+        before("g", R.split(), [])
+        for o, i in pairs:
+            g.remote_dma(o, i, T.sem[sem], T.sem["loc"], pid, rid, topo.mask(core, dst))
+            count["loc"] += len(topo.engines(core, dst))
+
+    def lands(key, src, sem, writes):
+        writer[key], readers[key] = ("far", sem, writes * len(topo.engines(src, core))), []
+
+    v = g.vector
+    cp, ts, tt, scan, qz = v.tensor_copy, v.tensor_scalar, v.tensor_tensor, v.tensor_tensor_scan, v.quantize_mx
+
+    def bank(b, n): return T.ps[:, 512 * b:512 * b + n]
+
+    def at(buf, a, b): return T[buf][:, a:b]
+
+    def mm(b, n, R, lhs, la, rhs, ra):
+        op("t", g.tensor.matmul_mx, R, "B%d" % b, bank(b, n), at(lhs + "q", la, la + 128), at(lhs + "s", la, la + 128),
+           at(rhs + "q", ra, ra + n), at(rhs + "s", ra, ra + n), True, True)
+
+    def pick(win, a, b, off, c=0, d=24): return T[win][:, a:b].indirect(T[off][:, c:d])
+
+    partner = [T.cores[rank ^ m] for m in MASK]
+
+    D("y", "", "sei", T.sei[:], T.se[:])
+    D("y", "", "x0.0", T.x0[:, 0:4 * CH[0][1]], T.x[:, 0:4 * CH[0][1]])
+    D("s", "", "ua", T.ua[:], T.u[:])
+    D("s", "", "x0.1", T.x0[:, 4 * CH[1][0]:4 * C], T.x[:, 4 * CH[1][0]:4 * C])
+    D("y", "", "ub", T.ub[:, 0:448], T.u[:, 64:512])
+    D("y", "", "ub2", T.ub[:, 448:512], T.u[:, 0:64])
+    D("y", "", "layq", T.layq[:, 0:512].bitcast(dt.uint8), T.wc[:, 0:2048])
+    D("y", "", "lays", T.lays[:, 0:512], T.ws[:, 0:512])
+    D("y", "", "vt", T.vt[:], T.v[:])
+
+    small = {"allow_small_or_imprecise_dtypes": True}
+
+    def iota(W, out, *a, **kw): op("g", g.iota, "", W, out, *a, **kw)
+    iota("idc", T.idc[:], [[1, C]], -192, 0, **small)
+    iota("ia", T.ia[:], [[1, C]], 128, -1)
+    iota("ip", T.ip[:], [[0, NB]], 0, 1)
+    iota("iq", T.iq[:], [[16, NB]], 0, 0)
+    iota("ib", T.ib[:], [[4, C]], 131, -1)
+    iota("i8", T.i8[:], [[16, 8]], 6, 0)
+    V(v.memset, "", "r16", T.r16[:], 1.0)
+    V(v.memset, "", "r4", T.r4[:], 1.0)
+    V(v.memset, "", "one", T.one[:], 1.0)
+    V(v.memset, "", "mm", T.mm[:], 0.0)
+    V(v.memset, "", "dl", T.dl[:], 0.0)
+    V(v.memset, "r16", "r16", T.r16[:, 0:768:16], 0.0)
+    V(v.memset, "r4", "r4", T.r4[:, 0:C:4], 0.0)
+    V(ts, "ia", "ia", T.ia[:], T.ia[:], 15, None, A.bitwise_and)
+    V(ts, "ia", "mk", T.mk[:], T.ia[:], 0.0, None, A.is_equal)
+
+    V(cp, "sei", "ls0", T.ls0[:, 0:24], T.sei[:, 24:48])
+    V(cp, "sei", "ls0b", T.ls0[:, 24:48], T.sei[:, 0:24])
+
+    def send_lists(r): send(partner[r], "ls%d ls%db" % (r, r), "n%d" % r, [(T["ll%d" % r][:], T["ls%d" % r][:])])
+    for r in range(3):
+        lands("ll%d" % r, partner[r], "n%d" % r, 1)
+        for c in range(2): lands("l%d.%d" % (r, c), partner[r], "h%d_%d" % (r, c), 2)
+    send_lists(0)
+    for b in range(4):
+        op("g", g.affine_select, "one", "et%d" % b, T["et%d" % b][:], T.one[:], [[-1, 512]], A.is_equal, 0.0, b, 4)
+
+    V(ts, "ip", "ya", T.ya[:], T.ip[:], 15, None, A.bitwise_and)
+    V(ts, "ip", "yb", T.yb[:], T.ip[:], 1, None, A.bitwise_and)
+    V(ts, "ip", "yi", T.yi[:], T.ip[:], 3, None, A.bitwise_and)
+    V(ts, "ib", "ib", T.ib[:], T.ib[:], 15, None, A.bitwise_and)
+    V(tt, "ya iq", "ci", T.ci[:], T.ya[:], T.iq[:], A.add)
+    V(ts, "yb", "pd", T.pd[:, 0:1], T.yb[:, 0:1], -2.0, 1.0, A.mult, A.add)
+    V(ts, "yb", "pm", T.pd[:, 1:2], T.yb[:, 0:1], 14.0, 1.0, A.mult, A.add)
+    V(ts, "yi", "pq", T.pq[:, 0:1], T.yi[:, 0:1], 768.0, None, A.add)
+    V(ts, "ib", "mk4", T.mk4[:], T.ib[:], 3.0, None, A.is_le)
+    V(cp, "i8", "o6", T.o6[:], T.i8[:])
+    for l in range(2): V(cp, "ci", "ci2.%d" % l, T.ci2[:, :, l], T.ci[:])
+
+    def prepare(R, s1, s0, base):
+        V(tt, R, "sm", T.sm[:], s1, s0, A.add)
+        V(tt, R, "df", T.df[:], s1, s0, A.subtract)
+        V(ts, "sm", "mm", T.mm[:, :, 0], T.sm[:], 0.5, base, A.mult, A.add)
+        V(ts, "df", "dl", T.dl[:, :, 0], T.df[:], 0.5, None, A.mult)
+        for l in (2, 3, 4):
+            V(ts, "sm", "mm", T.mm[:, :, l], T.sm[:], 0.5, base + 192.0, A.mult, A.add)
+            V(ts, "df", "dl", T.dl[:, :, l], T.df[:], 0.5, 192.0, A.mult, A.add)
+
+    def own_window(r, win, a, b):
+        S("%s ls%db" % (win, r), "sw", T.sw[:, 0:C], pick(win, a, a + C, "ls%d" % r, 24, 48), F.Identity, scale=Q, bias=192.0 * Q)
+        S("%s ls%d" % (win, r), "sw1", T.sw[:, C:768], pick(win, b, b + C, "ls%d" % r), F.Identity, scale=Q, bias=1216.0 * Q)
+
+    def sp_table(r): S("idc ll%d" % r, "sp", T.sp[:], pick("idc", 0, C, "ll%d" % r, 0, 48))
+
+    def t2_table(r, h, q):
+        if q == "s":
+            S("sp ll%d" % r, "t2.%d" % h, T.t2[:, 768 * h:768 * h + 768], pick("sp", C * h, C * h + C, "ll%d" % r, 0, 48))
+        else:
+            V(cp, "sp ll%d" % r, "t2.%d" % h, T.t2[:, 768 * h:768 * h + 768], pick("sp", C * h, C * h + C, "ll%d" % r, 0, 48))
+
+    own_window(0, "idc", 0, 0)
+    prepare("sei", T.sei[:, 24:48], T.sei[:, 0:24], 0.0)
+    V(qz, "ua", "pa", T.paq[:], T.pas[:], T.ua[:])
+    V(qz, "ub ub2", "pb", T.pbq[:], T.pbs[:], T.ub[:])
+
+    def pack_state(r, c):
+        a, b = CH[c]
+        n = b - a
+        V(qz, "x%d.%d" % (r, c), "xq.%d" % c, T.xq[:, a:b], T.xs[:, a:b], T["x%d" % r][:, 4 * a:4 * b])
+        if r == 3: return
+        mm(2 * c, n, "pa xq.%d" % c, "pa", 0, "x", a)
+        mm(2 * c + 1, n, "pb xq.%d" % c, "pb", 0, "x", a)
+
+    def signs(c):
+        a, b = CH[c]
+        for h in range(2):
+            S("B%d" % (2 * c + h), "bt.%d" % c, T.bt[:, a // 16:b // 16, 16 * h:16 * h + 16], bank(2 * c + h, b - a), F.Sign, bias=-(2.0 ** -93))
+
+    def turned(c):
+        a, b = CH[c]
+        V(v.transpose, "bt.%d" % c, "tr.%d" % c, T.tr[:, a // 16:b // 16, :], T.bt[:, a // 16:b // 16, :])
+
+    def half(r, c):
+        a, b = CH[c]
+        V(ts, "x%d.%d" % (r, c), "xh.%d" % c, T.xh[:, 4 * a:4 * b], T["x%d" % r][:, 4 * a:4 * b], 0.5, None, A.mult)
+
+    for c in range(2):
+        pack_state(0, c)
+        signs(c)
+    V(ts, "ia pm", "km", T.km[:], T.ia[:], T.pd[:, 1:2], None, A.is_equal)
+    V(tt, "mk km", "mkc", T.mkc[:], T.mk[:], T.km[:], A.subtract)
+    turned(0)
+    turned(1)
+
+    def take(win, R, off, mask, out, a=0, b=C, c=0, d=24, o=0):
+        V(tt, "%s %s" % (R, mask), out, T[out][:, o:o + C], pick(win, a, b, off, c, d), T[mask][:, 0:C], A.mult)
+
+    def gather_sum(src, out, r, n=C): V(scan, "%s %s" % (src, r), out, T[out][:, 0:n], T[r][:, 0:n], T[src][:, 0:n], 0.0, A.mult, A.add)
+
+    def last(buf, a=0, step=16): return T[buf][:, a + step - 1:a + C:step]
+
+    for r in range(3):
+        X, dst = "x%d" % r, partner[r]
+        TR = "tr.0 tr.1"
+        V(ts, TR, "e15", T.e15[:], T.tr[:, :, 1:6:4], 192.0, 192.0, A.mult, A.add)
+        V(tt, "e15 ci2.0 ci2.1", "e15", T.e15[:], T.e15[:], T.ci2[:], A.add)
+        V(cp, "e15", "o5", T.o5[:], T.e15[:, :, 1])
+        V(cp, "e15", "o1", T.o1[:], T.e15[:, :, 0])
+        S("sw sw1 o5", "rw5", T.rw5[:, 0:C], pick("sw", 0, 768, "o5"))
+        S("rw5", "rw5b", T.rw5[:, C:768], T.rw5[:, 0:C], F.Identity, bias=512.0 * Q)
+        V(tt, TR + " dl", "fm", T.fm[:], T.tr[:, :, 0:5], T.dl[:], A.mult)
+        V(tt, "fm mm", "fm", T.fm[:], T.fm[:], T.mm[:], A.add)
+        for l in (4, 0): V(cp, "fm", "o%d" % l, T["o%d" % l][:], T.fm[:, :, l])
+        S("rw5 rw5b o4", "rw4", T.rw4[:, 0:C], pick("rw5", 0, 768, "o4"))
+        S("rw4", "rw4b", T.rw4[:, C:768], T.rw4[:, 0:C], F.Identity, bias=768.0)
+        if r == 0:
+            sp_table(0)
+            t2_table(0, 1, "s")
+        V(cp, "sw sw1 o1", "a1", T.a1[:], pick("sw", 0, 768, "o1"))
+        for l in (3, 2): V(cp, "fm", "o%d" % l, T["o%d" % l][:], T.fm[:, :, l])
+        S("rw4 rw4b o3", "rw3", T.rw3[:, 0:C], pick("rw4", 0, 768, "o3"))
+        S("rw3", "rw3b", T.rw3[:, C:768], T.rw3[:, 0:C], F.Identity, bias=384.0)
+        take("a1", "a1 o0", "o0", "mk", "am")
+        V(ts, TR, "cb", T.cb[:], T.tr[:, :, 0], 192.0, 192.0, A.mult, A.add)
+        gather_sum("am", "an", "r16")
+        V(tt, "cb ci", "cb", T.cb[:], T.cb[:], T.ci[:], A.add)
+        S("rw3 rw3b o2", "rw2", T.rw2[:], pick("rw3", 0, 768, "o2"))
+        V(ts, "an", "hb", T.hb[:], last("an"), 1024.0 * Q, 768.0, A.is_ge, A.mult)
+        V(ts, "an", "ya", T.ya[:], last("an"), 1 / Q, None, A.mult)
+        V(tt, "hb cb", "hb", T.hb[:], T.hb[:], T.cb[:], A.add)
+        V(ts, "ya", "ya", T.ya[:], T.ya[:], 511, None, A.bitwise_and)
+        V(cp, "hb", "oa", T.oa[:], T.hb[:])
+        V(cp, "ya", "oi", T.oi[:], T.ya[:])
+        if r == 0:
+            t2_table(0, 0, "v")
+            V(cp, "pa o6", "p6", T.p6q[:, 0:128].bitcast(dt.uint32), T.paq[:, 0:128].bitcast(dt.uint32).indirect(T.o6[:, 0:8]))
+            V(cp, "pa o6", "p6s", T.p6s[:, 0:128], T.pas[:, 0:128].indirect(T.o6[:, 0:8]))
+        mm(4, C, "p6 p6s xq.0 xq.1", "p6", 0, "x", 0)
+        S("B4", "e6", T.e6[:], bank(4, C), F.Sign, bias=-(2.0 ** -93))
+        for c in range(2): half(r, c)
+        T2 = "t2.0 t2.1"
+        take("t2", T2 + " oa", "oa", "mk", "km", 0, 1536)
+        gather_sum("km", "ks", "r16")
+        V(ts, "ks", "k2", T.k2[:], last("ks"), 192.0, None, A.add)
+        take("rw2", "rw2 oi", "oi", "mk", "am")
+        gather_sum("am", "an", "r16")
+        V(tt, "an k2", "fk", T.fk[:], last("an"), T.k2[:], A.add)
+        V(ts, "an", "yb", T.yb[:], last("an"), 1 / Q, None, A.mult)
+        V(cp, "fk", "ob", T.ob[:], T.fk[:])
+        V(ts, "yb", "yi", T.yi[:], T.yb[:], 511, None, A.bitwise_and)
+        V(ts, "yb", "yw", T.yw[:], T.yb[:], 1536, None, A.bitwise_and)
+        for t in range(4): V(ts, "yi", "oi6.%d" % t, T.oi6[:, 24 * t:24 * t + 24], T.yi[:], 4.0, float(t), A.mult, A.add)
+        for c, (a, b) in enumerate(CH):
+            for t in range(4):
+                S("%s.0 %s.1 oi6.%d" % (X, X, t), "xi.%d.%d" % (c, t), T.xi[:, 4 * a + t:4 * b:4],
+                  pick(X, 0, 4 * C, "oi6", 24 * t + a // 16, 24 * t + b // 16), F.Copy, scale=0.5)
+        take("t2", T2 + " ob", "ob", "mk", "km", 0, 1536)
+        V(ts, "yw", "w4", T.w4[:], T.yw[:], 0.75, 192.0, A.mult, A.add)
+        gather_sum("km", "ks", "r16")
+        V(tt, "ks w4", "w4", T.w4[:], last("ks"), T.w4[:], A.add)
+        V(cp, "w4", "oc6", T.oc6[:], T.w4[:])
+        take("t2", T2 + " oc6", "oc6", "mk4", "km", 0, 1536)
+        gather_sum("km", "ks", "r4")
+        V(ts, "ks pq", "oz", T.oz[:], last("ks", 0, 4), 4.0, T.pq[:, 0:1], A.mult, A.add)
+        for c, (a, b) in enumerate(CH):
+            V(tt, "xh.0 xh.1 oz " + " ".join("xi.%d.%d" % (c, t) for t in range(4)), "zt.%d" % c, T.zt[:, 4 * a:4 * b],
+              pick("xh", 0, 4 * C, "oz", a // 4, b // 4), T.xi[:, 4 * a:4 * b], A.add)
+            V(qz, "zt.%d" % c, "z.%d" % c, T.zq[:, a:b], T.zs[:, a:b], T.zt[:, 4 * a:4 * b])
+            for k in range(4): mm(4 * c + k, b - a, "layq lays z.%d" % c, "lay", 128 * k, "z", a)
+
+        def layer(c, k, q):
+            a, b = CH[c]
+            o, W = T.ht[:, 4 * a + k:4 * b:4], "ht.%d.%d" % (c, k)
+            if q == "s": S("B%d" % (4 * c + k), W, o, bank(4 * c + k, b - a), F.Copy, scale=0.03125)
+            else: V(ts, "B%d" % (4 * c + k), W, o, bank(4 * c + k, b - a), 0.03125, None, A.mult)
+
+        def ship(c):
+            a, b = CH[c]
+            h, l = "h%d" % r, "l%d" % r
+            V(qz, " ".join("ht.%d.%d" % (c, k) for k in range(4)), "%s.%d" % (h, c), T[h + "q"][:, a:b], T[h + "s"][:, a:b], T.ht[:, 4 * a:4 * b])
+            send(dst, "%s.%d" % (h, c), "h%d_%d" % (r, c), [(T[l + "q"][:, a:b].bitcast(dt.uint8), T[h + "q"][:, a:b].bitcast(dt.uint8)),
+                                                         (T[l + "s"][:, a:b], T[h + "s"][:, a:b])])
+        for k in range(4): layer(0, k, "s")
+        ship(0)
+        take("t2", T2 + " oc6", "oc6", "mk", "km", 0, 1536)
+        for k in range(4): layer(1, k, "ssvv"[k])
+        ship(1)
+        gather_sum("km", "ks", "r16")
+        V(ts, "ks", "oe", T.oe[:], last("ks"), 192.0, None, A.add)
+        take("e6", "e6 oe", "oe", "mkc", "km")
+        gather_sum("km", "ks", "r16")
+        V(ts, "ks pd", "fe", T.fe[:], last("ks"), 0.0, T.pd[:, 0:1], A.not_equal, A.mult)
+        V(tt, "fe ci", "fe", T.fe[:], T.fe[:], T.ci[:], A.add)
+        V(cp, "fe", "ot", T.ot[:], T.fe[:])
+        S("sp ot", "yy", T.yy[:, 0:C], pick("sp", 0, C, "ot"))
+        V(cp, "sp ot", "yy1", T.yy[:, C:768], pick("sp", C, 768, "ot"))
+        L, N = "ls%d" % r, "ls%d" % (r + 1)
+        if r < 2:
+            V(tt, "yy1 %s mk" % L, "tm", T.tm[:, 0:C], pick("yy", C, 768, L), T.mk[:], A.mult)
+            V(tt, "yy %sb mk" % L, "tm1", T.tm[:, C:768], pick("yy", 0, C, L, 24, 48), T.mk[:], A.mult)
+            V(scan, "tm tm1 r16", "tn", T.tn[:], T.r16[:], T.tm[:], 0.0, A.mult, A.add)
+            V(ts, "tn", N + " " + N + "b", T[N][:], T.tn[:, 15:768:16], 192.0, None, A.add)
+            send_lists(r + 1)
+            S("yy %sb" % L, "sw", T.sw[:, 0:C], pick("yy", 0, C, L, 24, 48), F.Identity, scale=Q, bias=192.0 * Q)
+            S("yy1 %s" % L, "sw1", T.sw[:, C:768], pick("yy", C, 768, L), F.Identity, scale=Q, bias=1216.0 * Q)
+        V(tt, "yy %sb mk4" % L, "km", T.km[:], pick("yy", 0, C, L, 24, 48), T.mk4[:], A.mult)
+        gather_sum("km", "ks", "r4")
+        V(ts, "ks pq", "od", T.od[:], last("ks", 0, 4), 4.0, T.pq[:, 0:1], A.mult, A.add)
+        if r == 0:
+            for k in range(4): V(qz, "et%d" % k, "e%d" % k, T["e%dq" % k][:], T["e%ds" % k][:], T["et%d" % k][:])
+            V(qz, "vt", "pv", T.pvq[:], T.pvs[:], T.vt[:])
+        if r < 2: prepare("tn", T.tn[:, 15:C:16], T.tn[:, C + 15:768:16], 192.0)
+        for c, (a, b) in enumerate(CH):
+            for k in range(4): mm(4 * c + k, b - a, "e%d l%d.%d" % (k, r, c), "e%d" % k, 0, "l%d" % r, a)
+            for k in range(4):
+                o, W, B = T.dd[:, 4 * a + k:4 * b:4], "dd.%d.%d" % (c, k), "B%d" % (4 * c + k)
+                if c == 1 and k > 1: V(cp, B, W, o, bank(4 * c + k, b - a))
+                else: S(B, W, o, bank(4 * c + k, b - a))
+        if r < 2: sp_table(r + 1)
+        for c, (a, b) in enumerate(CH):
+            V(tt, "od %s.%d " % (X, c) + " ".join("dd.%d.%d" % (i, k) for i in range(2) for k in range(4)), "x%d.%d" % (r + 1, c),
+              T["x%d" % (r + 1)][:, 4 * a:4 * b], pick("dd", 0, 4 * C, "od", a // 4, b // 4), T[X][:, 4 * a:4 * b], A.add)
+            pack_state(r + 1, c)
+            if r < 2:
+                if c == 0: t2_table(r + 1, 0, "s")
+                signs(c)
+        if r < 2:
+            t2_table(r + 1, 1, "s")
+            turned(0)
+            turned(1)
+        else:
+            S("yy %sb" % L, "sod", T.sod[:, 0:C], pick("yy", 0, C, L, 24, 48), F.Identity, bias=192.0)
+            S("yy1 %s" % L, "sod1", T.sod[:, C:768], pick("yy", C, 768, L), F.Identity, bias=192.0)
+
+    ends = [D("y", "sod sod1", "", T["so"][:], T.sod[0:128:16, :])]
+    for c, (a, b) in enumerate(CH):
+        mm(c, b - a, "pv xq.%d" % c, "pv", 0, "x", a)
+        if c == 0: S("B%d" % c, "yd.%d" % c, T.yd[:, a:b], bank(c, b - a))
+        else: V(cp, "B%d" % c, "yd.%d" % c, T.yd[:, a:b], bank(c, b - a))
+    ends.append(D("y", "xq.0 xq.1", "", T.oc[:], T.xq[:].bitcast(dt.uint8)))
+    for k in range(4): ends.append(D("y" if k % 2 else "s", "xq.0 xq.1", "", T.osc[4 * k:4 * k + 4, 0:C], T.xs[32 * k:32 * k + 4, 0:C]))
+    ends.append(D("y", "yd.0 yd.1", "", T.y[:], T.yd[:]))
+    for s in ends: wait("y", s, 16)
+    for s in ("v", "s", "t", "i", "loc"): wait("g", s, count[s])

@@ -18,8 +18,10 @@ def _codes(names, n):
         _sb(k + "s", n, "uint8")
 
 
-_sb("ua ub vt et0 et1 et2 et3 one", 512, "bfloat16")
-_codes("pa pb p6 pv e0 e1 e2 e3", 128)
+_sb("ua", 576, "bfloat16")
+_sb("vt et0 et1 et2 et3 one", 512, "bfloat16")
+_codes("pa", 144)
+_codes("p6 pv e0 e1 e2 e3", 128)
 _codes("lay", 512)
 _sb("x0 x1 x2 x3 xh xi zt ht dd t2", 4 * C, "bfloat16")
 _codes("x z h0 h1 h2 l0 l1 l2", C)
@@ -30,7 +32,7 @@ _sb("idc mk mk4 mkc r4 km ks e6", C, "bfloat16")
 _sb("r16 sp yy tm tn", 768, "bfloat16")
 _sb("sw rw5 rw4 rw3 sod", 768, "float32")
 _sb("rw2 a1 am an yd", C, "float32")
-_sb("ia ib", C, "int32")
+_sb("ia ib ic", C, "int32")
 _sb("sei", 48, "int32")
 _sb("ip iq ya yb yi yw", 24, "int32")
 _sb("i8", 8, "int32")
@@ -93,15 +95,16 @@ def rank_program(g, core, T, topo):
         after("dma", s, 16, R, W)
         return s
 
-    def send(dst, R, sem, pairs):
+    def send(dst, R, sem, pairs, most=16):
         rid, pid, _ = topo.addr(dst)
         before("g", R.split(), [])
+        use = topo.engines(core, dst)[:most]
         for o, i in pairs:
-            g.remote_dma(o, i, T.sem[sem], T.sem["loc"], pid, rid, topo.mask(core, dst))
-            count["loc"] += len(topo.engines(core, dst))
+            g.remote_dma(o, i, T.sem[sem], T.sem["loc"], pid, rid, sum(1 << e for e in use))
+            count["loc"] += len(use)
 
-    def lands(key, src, sem, writes):
-        writer[key], readers[key] = ("far", sem, writes * len(topo.engines(src, core))), []
+    def lands(key, src, sem, writes, most=16):
+        writer[key], readers[key] = ("far", sem, writes * len(topo.engines(src, core)[:most])), []
 
     v = g.vector
     cp, ts, tt, scan, qz = v.tensor_copy, v.tensor_scalar, v.tensor_tensor, v.tensor_tensor_scan, v.quantize_mx
@@ -120,10 +123,9 @@ def rank_program(g, core, T, topo):
 
     D("y", "", "sei", T.sei[:], T.se[:])
     D("y", "", "x0.0", T.x0[:, 0:4 * CH[0][1]], T.x[:, 0:4 * CH[0][1]])
-    D("s", "", "ua", T.ua[:], T.u[:])
+    D("s", "", "ua", T.ua[:, 0:512], T.u[:])
     D("s", "", "x0.1", T.x0[:, 4 * CH[1][0]:4 * C], T.x[:, 4 * CH[1][0]:4 * C])
-    D("y", "", "ub", T.ub[:, 0:448], T.u[:, 64:512])
-    D("y", "", "ub2", T.ub[:, 448:512], T.u[:, 0:64])
+    D("y", "", "ua2", T.ua[:, 512:576], T.u[:, 0:64])
     D("y", "", "layq", T.layq[:, 0:512].bitcast(dt.uint8), T.wc[:, 0:2048])
     D("y", "", "lays", T.lays[:, 0:512], T.ws[:, 0:512])
     D("y", "", "vt", T.vt[:], T.v[:])
@@ -131,44 +133,38 @@ def rank_program(g, core, T, topo):
     small = {"allow_small_or_imprecise_dtypes": True}
 
     def iota(W, out, *a, **kw): op("g", g.iota, "", W, out, *a, **kw)
-    iota("idc", T.idc[:], [[1, C]], -192, 0, **small)
-    iota("ia", T.ia[:], [[1, C]], 128, -1)
     iota("ip", T.ip[:], [[0, NB]], 0, 1)
     iota("iq", T.iq[:], [[16, NB]], 0, 0)
-    iota("ib", T.ib[:], [[4, C]], 131, -1)
+    iota("idc", T.idc[:], [[1, C]], -192, 0, **small)
     iota("i8", T.i8[:], [[16, 8]], 6, 0)
+    iota("ia", T.ia[:], [[1, C]], 128, -1)
     V(v.memset, "", "r16", T.r16[:], 1.0)
-    V(v.memset, "", "r4", T.r4[:], 1.0)
-    V(v.memset, "", "one", T.one[:], 1.0)
+    V(ts, "ip", "ya", T.ya[:], T.ip[:], 15, None, A.bitwise_and)
+    V(ts, "ip", "yb", T.yb[:], T.ip[:], 1, None, A.bitwise_and)
+    V(ts, "ip", "yi", T.yi[:], T.ip[:], 3, None, A.bitwise_and)
+    V(tt, "ya iq", "ci", T.ci[:], T.ya[:], T.iq[:], A.add)
+    V(ts, "yb", "pd", T.pd[:, 0:1], T.yb[:, 0:1], -2.0, 1.0, A.mult, A.add)
+    V(ts, "yi", "pq", T.pq[:, 0:1], T.yi[:, 0:1], 768.0, None, A.add)
+    for l in range(2): V(cp, "ci", "ci2.%d" % l, T.ci2[:, :, l], T.ci[:])
     V(v.memset, "", "mm", T.mm[:], 0.0)
     V(v.memset, "", "dl", T.dl[:], 0.0)
     V(v.memset, "r16", "r16", T.r16[:, 0:768:16], 0.0)
+    V(v.memset, "", "one", T.one[:], 1.0)
+    V(v.memset, "", "r4", T.r4[:], 1.0)
     V(v.memset, "r4", "r4", T.r4[:, 0:C:4], 0.0)
-    V(ts, "ia", "ia", T.ia[:], T.ia[:], 15, None, A.bitwise_and)
-    V(ts, "ia", "mk", T.mk[:], T.ia[:], 0.0, None, A.is_equal)
 
     V(cp, "sei", "ls0", T.ls0[:, 0:24], T.sei[:, 24:48])
     V(cp, "sei", "ls0b", T.ls0[:, 24:48], T.sei[:, 0:24])
 
-    def send_lists(r): send(partner[r], "ls%d ls%db" % (r, r), "n%d" % r, [(T["ll%d" % r][:], T["ls%d" % r][:])])
+    def send_lists(r): send(partner[r], "ls%d ls%db" % (r, r), "n%d" % r, [(T["ll%d" % r][:], T["ls%d" % r][:])], 4)
     for r in range(3):
-        lands("ll%d" % r, partner[r], "n%d" % r, 1)
+        lands("ll%d" % r, partner[r], "n%d" % r, 1, 4)
         for c in range(2): lands("l%d.%d" % (r, c), partner[r], "h%d_%d" % (r, c), 2)
     send_lists(0)
+    iota("ib", T.ib[:], [[4, C]], 131, -1)
+    iota("ic", T.ic[:], [[2, C // 2], [0, 2]], 129, -1)
     for b in range(4):
         op("g", g.affine_select, "one", "et%d" % b, T["et%d" % b][:], T.one[:], [[-1, 512]], A.is_equal, 0.0, b, 4)
-
-    V(ts, "ip", "ya", T.ya[:], T.ip[:], 15, None, A.bitwise_and)
-    V(ts, "ip", "yb", T.yb[:], T.ip[:], 1, None, A.bitwise_and)
-    V(ts, "ip", "yi", T.yi[:], T.ip[:], 3, None, A.bitwise_and)
-    V(ts, "ib", "ib", T.ib[:], T.ib[:], 15, None, A.bitwise_and)
-    V(tt, "ya iq", "ci", T.ci[:], T.ya[:], T.iq[:], A.add)
-    V(ts, "yb", "pd", T.pd[:, 0:1], T.yb[:, 0:1], -2.0, 1.0, A.mult, A.add)
-    V(ts, "yb", "pm", T.pd[:, 1:2], T.yb[:, 0:1], 14.0, 1.0, A.mult, A.add)
-    V(ts, "yi", "pq", T.pq[:, 0:1], T.yi[:, 0:1], 768.0, None, A.add)
-    V(ts, "ib", "mk4", T.mk4[:], T.ib[:], 3.0, None, A.is_le)
-    V(cp, "i8", "o6", T.o6[:], T.i8[:])
-    for l in range(2): V(cp, "ci", "ci2.%d" % l, T.ci2[:, :, l], T.ci[:])
 
     def prepare(R, s1, s0, base):
         V(tt, R, "sm", T.sm[:], s1, s0, A.add)
@@ -185,16 +181,19 @@ def rank_program(g, core, T, topo):
 
     def sp_table(r): S("idc ll%d" % r, "sp", T.sp[:], pick("idc", 0, C, "ll%d" % r, 0, 48))
 
-    def t2_table(r, h, q):
-        if q == "s":
-            S("sp ll%d" % r, "t2.%d" % h, T.t2[:, 768 * h:768 * h + 768], pick("sp", C * h, C * h + C, "ll%d" % r, 0, 48))
-        else:
-            V(cp, "sp ll%d" % r, "t2.%d" % h, T.t2[:, 768 * h:768 * h + 768], pick("sp", C * h, C * h + C, "ll%d" % r, 0, 48))
+    def t2_table(r, q, p, n):
+        h = p // 2
+        a = ("sp ll%d" % r, " ".join("t2.%d" % k for k in range(p, p + n)), T.t2[:, C * p:C * (p + n)],
+             pick("sp", C * h, C * h + C, "ll%d" % r, 24 * (p % 2), 24 * (p % 2 + n)))
+        if q == "s": S(*a)
+        else: V(cp, *a)
 
     own_window(0, "idc", 0, 0)
-    prepare("sei", T.sei[:, 24:48], T.sei[:, 0:24], 0.0)
-    V(qz, "ua", "pa", T.paq[:], T.pas[:], T.ua[:])
-    V(qz, "ub ub2", "pb", T.pbq[:], T.pbs[:], T.ub[:])
+    V(ts, "ia", "ia", T.ia[:], T.ia[:], 15, None, A.bitwise_and)
+    V(qz, "ua ua2", "pa", T.paq[:, 0:144], T.pas[:, 0:144], T.ua[:, 0:576])
+    V(cp, "i8", "o6", T.o6[:], T.i8[:])
+    V(cp, "pa o6", "p6", T.p6q[:, 0:128].bitcast(dt.uint32), T.paq[:, 0:128].bitcast(dt.uint32).indirect(T.o6[:, 0:8]))
+    S("pa o6", "p6s", T.p6s[:, 0:128], T.pas[:, 0:128].indirect(T.o6[:, 0:8]))
 
     def pack_state(r, c):
         a, b = CH[c]
@@ -202,7 +201,7 @@ def rank_program(g, core, T, topo):
         V(qz, "x%d.%d" % (r, c), "xq.%d" % c, T.xq[:, a:b], T.xs[:, a:b], T["x%d" % r][:, 4 * a:4 * b])
         if r == 3: return
         mm(2 * c, n, "pa xq.%d" % c, "pa", 0, "x", a)
-        mm(2 * c + 1, n, "pb xq.%d" % c, "pb", 0, "x", a)
+        mm(2 * c + 1, n, "pa xq.%d" % c, "pa", 16, "x", a)
 
     def signs(c):
         a, b = CH[c]
@@ -215,13 +214,14 @@ def rank_program(g, core, T, topo):
 
     def half(r, c):
         a, b = CH[c]
-        V(ts, "x%d.%d" % (r, c), "xh.%d" % c, T.xh[:, 4 * a:4 * b], T["x%d" % r][:, 4 * a:4 * b], 0.5, None, A.mult)
+        o, i = T.xh[:, 4 * a:4 * b], T["x%d" % r][:, 4 * a:4 * b]
+        S("x%d.%d" % (r, c), "xh.%d" % c, o, i, F.Copy, scale=0.5)
 
     for c in range(2):
         pack_state(0, c)
         signs(c)
-    V(ts, "ia pm", "km", T.km[:], T.ia[:], T.pd[:, 1:2], None, A.is_equal)
-    V(tt, "mk km", "mkc", T.mkc[:], T.mk[:], T.km[:], A.subtract)
+    prepare("sei", T.sei[:, 24:48], T.sei[:, 0:24], 0.0)
+    V(ts, "ia", "mk", T.mk[:], T.ia[:], 0.0, None, A.is_equal)
     turned(0)
     turned(1)
 
@@ -237,27 +237,28 @@ def rank_program(g, core, T, topo):
         TR = "tr.0 tr.1"
         V(ts, TR, "e15", T.e15[:], T.tr[:, :, 1:6:4], 192.0, 192.0, A.mult, A.add)
         V(tt, "e15 ci2.0 ci2.1", "e15", T.e15[:], T.e15[:], T.ci2[:], A.add)
+        V(ts, TR, "cb", T.cb[:], T.tr[:, :, 0], 192.0, 192.0, A.mult, A.add)
         V(cp, "e15", "o5", T.o5[:], T.e15[:, :, 1])
         V(cp, "e15", "o1", T.o1[:], T.e15[:, :, 0])
         S("sw sw1 o5", "rw5", T.rw5[:, 0:C], pick("sw", 0, 768, "o5"))
         S("rw5", "rw5b", T.rw5[:, C:768], T.rw5[:, 0:C], F.Identity, bias=512.0 * Q)
         V(tt, TR + " dl", "fm", T.fm[:], T.tr[:, :, 0:5], T.dl[:], A.mult)
         V(tt, "fm mm", "fm", T.fm[:], T.fm[:], T.mm[:], A.add)
+        V(tt, "cb ci", "cb", T.cb[:], T.cb[:], T.ci[:], A.add)
         for l in (4, 0): V(cp, "fm", "o%d" % l, T["o%d" % l][:], T.fm[:, :, l])
         S("rw5 rw5b o4", "rw4", T.rw4[:, 0:C], pick("rw5", 0, 768, "o4"))
         S("rw4", "rw4b", T.rw4[:, C:768], T.rw4[:, 0:C], F.Identity, bias=768.0)
         if r == 0:
             sp_table(0)
-            t2_table(0, 1, "s")
+            t2_table(0, "s", 2, 2)
         V(cp, "sw sw1 o1", "a1", T.a1[:], pick("sw", 0, 768, "o1"))
-        for l in (3, 2): V(cp, "fm", "o%d" % l, T["o%d" % l][:], T.fm[:, :, l])
+        V(cp, "fm", "o3", T.o3[:], T.fm[:, :, 3])
         S("rw4 rw4b o3", "rw3", T.rw3[:, 0:C], pick("rw4", 0, 768, "o3"))
         S("rw3", "rw3b", T.rw3[:, C:768], T.rw3[:, 0:C], F.Identity, bias=384.0)
         take("a1", "a1 o0", "o0", "mk", "am")
-        V(ts, TR, "cb", T.cb[:], T.tr[:, :, 0], 192.0, 192.0, A.mult, A.add)
+        V(cp, "fm", "o2", T.o2[:], T.fm[:, :, 2])
         gather_sum("am", "an", "r16")
-        V(tt, "cb ci", "cb", T.cb[:], T.cb[:], T.ci[:], A.add)
-        S("rw3 rw3b o2", "rw2", T.rw2[:], pick("rw3", 0, 768, "o2"))
+        S("rw3 rw3b o2", "rw2", T.rw2[:], pick("rw3", 0, 768, "o2"), F.Identity, bias=192.0)
         V(ts, "an", "hb", T.hb[:], last("an"), 1024.0 * Q, 768.0, A.is_ge, A.mult)
         V(ts, "an", "ya", T.ya[:], last("an"), 1 / Q, None, A.mult)
         V(tt, "hb cb", "hb", T.hb[:], T.hb[:], T.cb[:], A.add)
@@ -265,29 +266,34 @@ def rank_program(g, core, T, topo):
         V(cp, "hb", "oa", T.oa[:], T.hb[:])
         V(cp, "ya", "oi", T.oi[:], T.ya[:])
         if r == 0:
-            t2_table(0, 0, "v")
-            V(cp, "pa o6", "p6", T.p6q[:, 0:128].bitcast(dt.uint32), T.paq[:, 0:128].bitcast(dt.uint32).indirect(T.o6[:, 0:8]))
-            V(cp, "pa o6", "p6s", T.p6s[:, 0:128], T.pas[:, 0:128].indirect(T.o6[:, 0:8]))
-        mm(4, C, "p6 p6s xq.0 xq.1", "p6", 0, "x", 0)
-        S("B4", "e6", T.e6[:], bank(4, C), F.Sign, bias=-(2.0 ** -93))
+            V(ts, "ib", "ib", T.ib[:], T.ib[:], 15, None, A.bitwise_and)
+            t2_table(0, "v", 0, 2)
         for c in range(2): half(r, c)
-        T2 = "t2.0 t2.1"
-        take("t2", T2 + " oa", "oa", "mk", "km", 0, 1536)
-        gather_sum("km", "ks", "r16")
-        V(ts, "ks", "k2", T.k2[:], last("ks"), 192.0, None, A.add)
+        T2 = "t2.0 t2.1 t2.2 t2.3"
+
+        def first_two():
+            take("t2", T2 + " oa", "oa", "mk", "km", 0, 1536)
+            gather_sum("km", "ks", "r16")
+
+        def own_ends(t): V(ts, "yi", "oi6.%d" % t, T.oi6[:, 24 * t:24 * t + 24], T.yi[:], 4.0, float(t), A.mult, A.add)
+        first_two()
+        if r == 0:
+            V(ts, "ib", "mk4", T.mk4[:], T.ib[:], 3.0, None, A.is_le)
+            V(ts, "ic", "ic", T.ic[:], T.ic[:], 15, None, A.bitwise_and)
         take("rw2", "rw2 oi", "oi", "mk", "am")
         gather_sum("am", "an", "r16")
-        V(tt, "an k2", "fk", T.fk[:], last("an"), T.k2[:], A.add)
         V(ts, "an", "yb", T.yb[:], last("an"), 1 / Q, None, A.mult)
-        V(cp, "fk", "ob", T.ob[:], T.fk[:])
+        V(tt, "an ks", "fk", T.fk[:], last("an"), last("ks"), A.add)
         V(ts, "yb", "yi", T.yi[:], T.yb[:], 511, None, A.bitwise_and)
         V(ts, "yb", "yw", T.yw[:], T.yb[:], 1536, None, A.bitwise_and)
-        for t in range(4): V(ts, "yi", "oi6.%d" % t, T.oi6[:, 24 * t:24 * t + 24], T.yi[:], 4.0, float(t), A.mult, A.add)
+        V(cp, "fk", "ob", T.ob[:], T.fk[:])
+        for t in (0, 1): own_ends(t)
+        take("t2", T2 + " ob", "ob", "mk", "km", 0, 1536)
+        for t in (2, 3): own_ends(t)
         for c, (a, b) in enumerate(CH):
             for t in range(4):
                 S("%s.0 %s.1 oi6.%d" % (X, X, t), "xi.%d.%d" % (c, t), T.xi[:, 4 * a + t:4 * b:4],
                   pick(X, 0, 4 * C, "oi6", 24 * t + a // 16, 24 * t + b // 16), F.Copy, scale=0.5)
-        take("t2", T2 + " ob", "ob", "mk", "km", 0, 1536)
         V(ts, "yw", "w4", T.w4[:], T.yw[:], 0.75, 192.0, A.mult, A.add)
         gather_sum("km", "ks", "r16")
         V(tt, "ks w4", "w4", T.w4[:], last("ks"), T.w4[:], A.add)
@@ -295,34 +301,40 @@ def rank_program(g, core, T, topo):
         take("t2", T2 + " oc6", "oc6", "mk4", "km", 0, 1536)
         gather_sum("km", "ks", "r4")
         V(ts, "ks pq", "oz", T.oz[:], last("ks", 0, 4), 4.0, T.pq[:, 0:1], A.mult, A.add)
-        for c, (a, b) in enumerate(CH):
-            V(tt, "xh.0 xh.1 oz " + " ".join("xi.%d.%d" % (c, t) for t in range(4)), "zt.%d" % c, T.zt[:, 4 * a:4 * b],
-              pick("xh", 0, 4 * C, "oz", a // 4, b // 4), T.xi[:, 4 * a:4 * b], A.add)
-            V(qz, "zt.%d" % c, "z.%d" % c, T.zq[:, a:b], T.zs[:, a:b], T.zt[:, 4 * a:4 * b])
-            for k in range(4): mm(4 * c + k, b - a, "layq lays z.%d" % c, "lay", 128 * k, "z", a)
+        def layer(z, k, q):
+            o, W, B = T.ht[:, 512 * z + k:512 * z + 512:4], "ht.%d.%d" % (z, k), 4 * (z % 2) + k
+            if q == "s": S("B%d" % B, W, o, bank(B, 128), F.Copy, scale=0.03125)
+            else: V(ts, "B%d" % B, W, o, bank(B, 128), 0.03125, None, A.mult)
 
-        def layer(c, k, q):
-            a, b = CH[c]
-            o, W = T.ht[:, 4 * a + k:4 * b:4], "ht.%d.%d" % (c, k)
-            if q == "s": S("B%d" % (4 * c + k), W, o, bank(4 * c + k, b - a), F.Copy, scale=0.03125)
-            else: V(ts, "B%d" % (4 * c + k), W, o, bank(4 * c + k, b - a), 0.03125, None, A.mult)
+        for z in range(3):
+            a = 128 * z
+            V(tt, "xh.0 xh.1 oz " + " ".join("xi.%d.%d" % (z // 2, t) for t in range(4)), "zt.%d" % z, T.zt[:, 4 * a:4 * a + 512],
+              pick("xh", 0, 4 * C, "oz", a // 4, a // 4 + 32), T.xi[:, 4 * a:4 * a + 512], A.add)
+            V(qz, "zt.%d" % z, "z.%d" % z, T.zq[:, a:a + 128], T.zs[:, a:a + 128], T.zt[:, 4 * a:4 * a + 512])
+            for k in range(4): mm(4 * (z % 2) + k, 128, "layq lays z.%d" % z, "lay", 128 * k, "z", a)
+            if z < 2:
+                for k in range(4): layer(z, k, "s")
+        if r == 0:
+            V(ts, "ic", "mkc", T.mkc[:], T.ic[:], 1.0, None, A.is_le)
 
         def ship(c):
             a, b = CH[c]
             h, l = "h%d" % r, "l%d" % r
-            V(qz, " ".join("ht.%d.%d" % (c, k) for k in range(4)), "%s.%d" % (h, c), T[h + "q"][:, a:b], T[h + "s"][:, a:b], T.ht[:, 4 * a:4 * b])
+            V(qz, " ".join("ht.%d.%d" % (z, k) for z in range(a // 128, b // 128) for k in range(4)), "%s.%d" % (h, c),
+              T[h + "q"][:, a:b], T[h + "s"][:, a:b], T.ht[:, 4 * a:4 * b])
             send(dst, "%s.%d" % (h, c), "h%d_%d" % (r, c), [(T[l + "q"][:, a:b].bitcast(dt.uint8), T[h + "q"][:, a:b].bitcast(dt.uint8)),
                                                          (T[l + "s"][:, a:b], T[h + "s"][:, a:b])])
-        for k in range(4): layer(0, k, "s")
         ship(0)
         take("t2", T2 + " oc6", "oc6", "mk", "km", 0, 1536)
-        for k in range(4): layer(1, k, "ssvv"[k])
-        ship(1)
+        mm(4, C, "p6 p6s xq.0 xq.1", "p6", 0, "x", 0)
+        for k in range(4): layer(2, k, "s")
+        S("B4", "e6", T.e6[:], bank(4, C), F.Sign, bias=-(2.0 ** -93))
         gather_sum("km", "ks", "r16")
+        ship(1)
         V(ts, "ks", "oe", T.oe[:], last("ks"), 192.0, None, A.add)
         take("e6", "e6 oe", "oe", "mkc", "km")
         gather_sum("km", "ks", "r16")
-        V(ts, "ks pd", "fe", T.fe[:], last("ks"), 0.0, T.pd[:, 0:1], A.not_equal, A.mult)
+        V(ts, "ks pd", "fe", T.fe[:], last("ks"), 0.0, T.pd[:, 0:1], A.is_equal, A.mult)
         V(tt, "fe ci", "fe", T.fe[:], T.fe[:], T.ci[:], A.add)
         V(cp, "fe", "ot", T.ot[:], T.fe[:])
         S("sp ot", "yy", T.yy[:, 0:C], pick("sp", 0, C, "ot"))
@@ -350,28 +362,31 @@ def rank_program(g, core, T, topo):
                 if c == 1 and k > 1: V(cp, B, W, o, bank(4 * c + k, b - a))
                 else: S(B, W, o, bank(4 * c + k, b - a))
         if r < 2: sp_table(r + 1)
+        else:
+            S("yy %sb" % L, "sod", T.sod[:, 0:C], pick("yy", 0, C, L, 24, 48), F.Identity, bias=192.0)
+            S("yy1 %s" % L, "sod1", T.sod[:, C:768], pick("yy", C, 768, L), F.Identity, bias=192.0)
+            ends = [D("g", "sod sod1", "", T["so"][:], T.sod[0:128:16, :])]
         for c, (a, b) in enumerate(CH):
             V(tt, "od %s.%d " % (X, c) + " ".join("dd.%d.%d" % (i, k) for i in range(2) for k in range(4)), "x%d.%d" % (r + 1, c),
               T["x%d" % (r + 1)][:, 4 * a:4 * b], pick("dd", 0, 4 * C, "od", a // 4, b // 4), T[X][:, 4 * a:4 * b], A.add)
             pack_state(r + 1, c)
             if r < 2:
-                if c == 0: t2_table(r + 1, 0, "s")
+                if c == 0: t2_table(r + 1, "s", 0, 2)
                 signs(c)
+            else:
+                mm(c, b - a, "pv xq.%d" % c, "pv", 0, "x", a)
+                if c == 0: S("B0", "yd.0", T.yd[:, a:b], bank(0, b - a))
+                else: V(cp, "B1", "yd.1", T.yd[:, a:b], bank(1, b - a))
+                ends.append(D("y", "xq.%d" % c, "", T.oc[:, 4 * a:4 * b], T.xq[:, a:b].bitcast(dt.uint8)))
+                if c == 1:
+                    for k in range(4):
+                        ends.append(D("ssyg"[k], "xq.0 xq.1", "", T.osc[4 * k:4 * k + 4, 0:C], T.xs[32 * k:32 * k + 4, 0:C]))
+                ends.append(D("y", "yd.%d" % c, "", T.y[:, a:b], T.yd[:, a:b]))
         if r < 2:
-            t2_table(r + 1, 1, "s")
+            t2_table(r + 1, "v", 3, 1)
+            t2_table(r + 1, "s", 2, 1)
             turned(0)
             turned(1)
-        else:
-            S("yy %sb" % L, "sod", T.sod[:, 0:C], pick("yy", 0, C, L, 24, 48), F.Identity, bias=192.0)
-            S("yy1 %s" % L, "sod1", T.sod[:, C:768], pick("yy", C, 768, L), F.Identity, bias=192.0)
 
-    ends = [D("y", "sod sod1", "", T["so"][:], T.sod[0:128:16, :])]
-    for c, (a, b) in enumerate(CH):
-        mm(c, b - a, "pv xq.%d" % c, "pv", 0, "x", a)
-        if c == 0: S("B%d" % c, "yd.%d" % c, T.yd[:, a:b], bank(c, b - a))
-        else: V(cp, "B%d" % c, "yd.%d" % c, T.yd[:, a:b], bank(c, b - a))
-    ends.append(D("y", "xq.0 xq.1", "", T.oc[:], T.xq[:].bitcast(dt.uint8)))
-    for k in range(4): ends.append(D("y" if k % 2 else "s", "xq.0 xq.1", "", T.osc[4 * k:4 * k + 4, 0:C], T.xs[32 * k:32 * k + 4, 0:C]))
-    ends.append(D("y", "yd.0 yd.1", "", T.y[:], T.yd[:]))
     for s in ends: wait("y", s, 16)
     for s in ("v", "s", "t", "i", "loc"): wait("g", s, count[s])

from concourse.mybir import dt, AluOpType, ActivationFunctionType

C = 384
NB = C // 16
MASK = [1, 2, 4]
CH = [(0, 256), (256, 384)]
Q = 2.0 ** -13
SCRATCH, SEMAPHORES = {}, ["v", "s", "t", "i", "loc"]


def _sb(names, n, dtype, *more):
    for k in names.split(): SCRATCH[k] = ("sbuf", [128, n] + list(more), dtype)


def _codes(names, n):
    for k in names.split():
        _sb(k + "q", n, "float8_e4m3fn_x4")
        _sb(k + "s", n, "uint8")


_sb("ua", 576, "bfloat16")
_sb("vt et0 et1 et2 et3 one", 512, "bfloat16")
_codes("pa", 144)
_codes("p6 pv e0 e1 e2 e3", 128)
_codes("lay", 512)
_sb("x0 x1 x2 x3 xh xi zt ht dd t2", 4 * C, "bfloat16")
_codes("x z h0 h1 h2 l0 l1 l2", C)
_sb("ll0 ll1 ll2 ls0 ls1 ls2 ls3", 48, "uint16")
SCRATCH["ps"] = ("psum", [128, 4096], "float32")
_sb("bt tr", NB, "bfloat16", 32)
_sb("idc mk mk4 mkc r4 km ks e6", C, "bfloat16")
_sb("r16 sp yy tm tn", 768, "bfloat16")
_sb("sw rw5 rw4 rw3 sod", 768, "float32")
_sb("rw2 a1 am an yd", C, "float32")
_sb("ia ib ic", C, "int32")
_sb("sei", 48, "int32")
_sb("ip iq ya yb yi yw", 24, "int32")
_sb("i8", 8, "int32")
_sb("ci cb hb fk k2 w4 fe sm df", 24, "float32")
_sb("pq pd", 2, "float32")
_sb("ci2 e15", NB, "float32", 2)
_sb("dl mm fm", NB, "float32", 5)
_sb("o0 o1 o2 o3 o4 o5 oa oi ob oc6 oe ot", 24, "uint16")
_sb("oi6 oz od", 96, "uint16")
_sb("o6", 8, "uint16")
SEMAPHORES += ["d%d" % k for k in range(20)]
SEMAPHORES += ["h%d_%d" % (r, c) for r in range(3) for c in range(2)] + ["n%d" % r for r in range(3)]


def rank_program(g, core, T, topo):
    rank = T.rank_of(core)
    if rank is None:
        return
    A, F = AluOpType, ActivationFunctionType
    queue = {"v": g.vector, "s": g.scalar, "t": g.tensor, "g": g, "y": g.sync}
    count = {"v": 0, "s": 0, "t": 0, "i": 0, "d": 0, "loc": 0}
    waited, writer, readers = {}, {}, {}

    def wait(q, s, n):
        if waited.get((q, s), 0) < n:
            queue[q].wait_ge(T.sem[s], n)
            waited[(q, s)] = n

    def before(q, R, W):
        need = {}
        for k in R:
            if k in writer: need[writer[k][1]] = max(need.get(writer[k][1], 0), writer[k][2])
        for k in W:
            for o in ([writer[k]] if k in writer else []) + readers.get(k, []):
                if o[0] != q: need[o[1]] = max(need.get(o[1], 0), o[2])
        for s in need: wait(q, s, need[s])

    def after(q, s, n, R, W):
        for k in W: writer[k], readers[k] = (q, s, n), []
        for k in R: readers.setdefault(k, []).append((q, s, n))

    def op(q, call, R, W, *a, **kw):
        R, W = R.split(), W.split()
        before(q, R, W)
        s = "i" if q == "g" else q
        call(*a, **kw).then_inc(T.sem[s], 1)
        count[s] += 1
        after(q, s, count[s], R, W)

    def V(call, R, W, *a): op("v", call, R, W, *a)

    def S(R, W, out, in_, func=F.Copy, **kw): op("s", g.scalar.activation, R, W, out, in_, func, **kw)

    def D(q, R, W, out, in_):
        R, W = R.split(), W.split()
        before(q, R, W)
        s = "d%d" % count["d"]
        count["d"] += 1
        queue[q].dma_start(out, in_).then_inc(T.sem[s], 16)
        after("dma", s, 16, R, W)
        return s

    def send(dst, R, sem, pairs, most=16):
        rid, pid, _ = topo.addr(dst)
        before("g", R.split(), [])
        use = topo.engines(core, dst)[:most]
        for o, i in pairs:
            g.remote_dma(o, i, T.sem[sem], T.sem["loc"], pid, rid, sum(1 << e for e in use))
            count["loc"] += len(use)

    def lands(key, src, sem, writes, most=16):
        writer[key], readers[key] = ("far", sem, writes * len(topo.engines(src, core)[:most])), []

    v = g.vector
    cp, ts, tt, scan, qz = v.tensor_copy, v.tensor_scalar, v.tensor_tensor, v.tensor_tensor_scan, v.quantize_mx

    def bank(b, n): return T.ps[:, 512 * b:512 * b + n]

    def at(buf, a, b): return T[buf][:, a:b]

    def mm(b, n, R, lhs, la, rhs, ra):
        op("t", g.tensor.matmul_mx, R, "B%d" % b, bank(b, n), at(lhs + "q", la, la + 128), at(lhs + "s", la, la + 128),
           at(rhs + "q", ra, ra + n), at(rhs + "s", ra, ra + n), True, True)

    def pick(win, a, b, off, c=0, d=24): return T[win][:, a:b].indirect(T[off][:, c:d])

    partner = [T.cores[rank ^ m] for m in MASK]

    D("y", "", "sei", T.sei[:], T.se[:])
    D("y", "", "x0.0", T.x0[:, 0:4 * CH[0][1]], T.x[:, 0:4 * CH[0][1]])
    D("s", "", "ua", T.ua[:, 0:512], T.u[:])
    D("s", "", "x0.1", T.x0[:, 4 * CH[1][0]:4 * C], T.x[:, 4 * CH[1][0]:4 * C])
    D("y", "", "ua2", T.ua[:, 512:576], T.u[:, 0:64])
    D("y", "", "layq", T.layq[:, 0:512].bitcast(dt.uint8), T.wc[:, 0:2048])
    D("y", "", "lays", T.lays[:, 0:512], T.ws[:, 0:512])
    D("y", "", "vt", T.vt[:], T.v[:])

    small = {"allow_small_or_imprecise_dtypes": True}

    def iota(W, out, *a, **kw): op("g", g.iota, "", W, out, *a, **kw)
    iota("ip", T.ip[:], [[0, NB]], 0, 1)
    iota("iq", T.iq[:], [[16, NB]], 0, 0)
    iota("idc", T.idc[:], [[1, C]], -192, 0, **small)
    iota("i8", T.i8[:], [[16, 8]], 6, 0)
    iota("ia", T.ia[:], [[1, C]], 128, -1)
    V(v.memset, "", "r16", T.r16[:], 1.0)
    V(ts, "ip", "ya", T.ya[:], T.ip[:], 15, None, A.bitwise_and)
    V(ts, "ip", "yb", T.yb[:], T.ip[:], 1, None, A.bitwise_and)
    V(ts, "ip", "yi", T.yi[:], T.ip[:], 3, None, A.bitwise_and)
    V(tt, "ya iq", "ci", T.ci[:], T.ya[:], T.iq[:], A.add)
    V(ts, "yb", "pd", T.pd[:, 0:1], T.yb[:, 0:1], -2.0, 1.0, A.mult, A.add)
    V(ts, "yi", "pq", T.pq[:, 0:1], T.yi[:, 0:1], 768.0, None, A.add)
    for l in range(2): V(cp, "ci", "ci2.%d" % l, T.ci2[:, :, l], T.ci[:])
    V(v.memset, "", "mm", T.mm[:], 0.0)
    V(v.memset, "", "dl", T.dl[:], 0.0)
    V(v.memset, "r16", "r16", T.r16[:, 0:768:16], 0.0)
    V(v.memset, "", "one", T.one[:], 1.0)
    V(v.memset, "", "r4", T.r4[:], 1.0)
    V(v.memset, "r4", "r4", T.r4[:, 0:C:4], 0.0)

    V(cp, "sei", "ls0", T.ls0[:, 0:24], T.sei[:, 24:48])
    V(cp, "sei", "ls0b", T.ls0[:, 24:48], T.sei[:, 0:24])

    def send_lists(r): send(partner[r], "ls%d ls%db" % (r, r), "n%d" % r, [(T["ll%d" % r][:], T["ls%d" % r][:])], 4)
    for r in range(3):
        lands("ll%d" % r, partner[r], "n%d" % r, 1, 4)
        for c in range(2): lands("l%d.%d" % (r, c), partner[r], "h%d_%d" % (r, c), 2)
    send_lists(0)
    iota("ib", T.ib[:], [[4, C]], 131, -1)
    iota("ic", T.ic[:], [[2, C // 2], [0, 2]], 129, -1)
    for b in range(4):
        op("g", g.affine_select, "one", "et%d" % b, T["et%d" % b][:], T.one[:], [[-1, 512]], A.is_equal, 0.0, b, 4)

    def prepare(R, s1, s0, base):
        V(tt, R, "sm", T.sm[:], s1, s0, A.add)
        V(tt, R, "df", T.df[:], s1, s0, A.subtract)
        V(ts, "sm", "mm", T.mm[:, :, 0], T.sm[:], 0.5, base, A.mult, A.add)
        V(ts, "df", "dl", T.dl[:, :, 0], T.df[:], 0.5, None, A.mult)
        for l in (2, 3, 4):
            V(ts, "sm", "mm", T.mm[:, :, l], T.sm[:], 0.5, base + 192.0, A.mult, A.add)
            V(ts, "df", "dl", T.dl[:, :, l], T.df[:], 0.5, 192.0, A.mult, A.add)

    def own_window(r, win, a, b):
        S("%s ls%db" % (win, r), "sw", T.sw[:, 0:C], pick(win, a, a + C, "ls%d" % r, 24, 48), F.Identity, scale=Q, bias=192.0 * Q)
        S("%s ls%d" % (win, r), "sw1", T.sw[:, C:768], pick(win, b, b + C, "ls%d" % r), F.Identity, scale=Q, bias=1216.0 * Q)

    def sp_table(r): S("idc ll%d" % r, "sp", T.sp[:], pick("idc", 0, C, "ll%d" % r, 0, 48))

    def t2_table(r, q, p, n):
        h = p // 2
        a = ("sp ll%d" % r, " ".join("t2.%d" % k for k in range(p, p + n)), T.t2[:, C * p:C * (p + n)],
             pick("sp", C * h, C * h + C, "ll%d" % r, 24 * (p % 2), 24 * (p % 2 + n)))
        if q == "s": S(*a)
        else: V(cp, *a)

    own_window(0, "idc", 0, 0)
    V(ts, "ia", "ia", T.ia[:], T.ia[:], 15, None, A.bitwise_and)
    V(qz, "ua ua2", "pa", T.paq[:, 0:144], T.pas[:, 0:144], T.ua[:, 0:576])
    V(cp, "i8", "o6", T.o6[:], T.i8[:])
    V(cp, "pa o6", "p6", T.p6q[:, 0:128].bitcast(dt.uint32), T.paq[:, 0:128].bitcast(dt.uint32).indirect(T.o6[:, 0:8]))
    S("pa o6", "p6s", T.p6s[:, 0:128], T.pas[:, 0:128].indirect(T.o6[:, 0:8]))

    def pack_state(r, c):
        a, b = CH[c]
        n = b - a
        V(qz, "x%d.%d" % (r, c), "xq.%d" % c, T.xq[:, a:b], T.xs[:, a:b], T["x%d" % r][:, 4 * a:4 * b])
        if r == 3: return
        mm(2 * c, n, "pa xq.%d" % c, "pa", 0, "x", a)
        mm(2 * c + 1, n, "pa xq.%d" % c, "pa", 16, "x", a)

    def signs(c):
        a, b = CH[c]
        for h in range(2):
            S("B%d" % (2 * c + h), "bt.%d" % c, T.bt[:, a // 16:b // 16, 16 * h:16 * h + 16], bank(2 * c + h, b - a), F.Sign, bias=-(2.0 ** -93))

    def turned(c):
        a, b = CH[c]
        V(v.transpose, "bt.%d" % c, "tr.%d" % c, T.tr[:, a // 16:b // 16, :], T.bt[:, a // 16:b // 16, :])

    def half(r, c):
        a, b = CH[c]
        o, i = T.xh[:, 4 * a:4 * b], T["x%d" % r][:, 4 * a:4 * b]
        S("x%d.%d" % (r, c), "xh.%d" % c, o, i, F.Copy, scale=0.5)

    for c in range(2):
        pack_state(0, c)
        signs(c)
    prepare("sei", T.sei[:, 24:48], T.sei[:, 0:24], 0.0)
    V(ts, "ia", "mk", T.mk[:], T.ia[:], 0.0, None, A.is_equal)
    turned(0)
    turned(1)

    def take(win, R, off, mask, out, a=0, b=C, c=0, d=24, o=0):
        V(tt, "%s %s" % (R, mask), out, T[out][:, o:o + C], pick(win, a, b, off, c, d), T[mask][:, 0:C], A.mult)

    def gather_sum(src, out, r, n=C): V(scan, "%s %s" % (src, r), out, T[out][:, 0:n], T[r][:, 0:n], T[src][:, 0:n], 0.0, A.mult, A.add)

    def last(buf, a=0, step=16): return T[buf][:, a + step - 1:a + C:step]

    for r in range(3):
        X, dst = "x%d" % r, partner[r]
        TR = "tr.0 tr.1"
        V(ts, TR, "e15", T.e15[:], T.tr[:, :, 1:6:4], 192.0, 192.0, A.mult, A.add)
        V(tt, "e15 ci2.0 ci2.1", "e15", T.e15[:], T.e15[:], T.ci2[:], A.add)
        V(ts, TR, "cb", T.cb[:], T.tr[:, :, 0], 192.0, 192.0, A.mult, A.add)
        V(cp, "e15", "o5", T.o5[:], T.e15[:, :, 1])
        V(cp, "e15", "o1", T.o1[:], T.e15[:, :, 0])
        S("sw sw1 o5", "rw5", T.rw5[:, 0:C], pick("sw", 0, 768, "o5"))
        S("rw5", "rw5b", T.rw5[:, C:768], T.rw5[:, 0:C], F.Identity, bias=512.0 * Q)
        V(tt, TR + " dl", "fm", T.fm[:], T.tr[:, :, 0:5], T.dl[:], A.mult)
        V(tt, "fm mm", "fm", T.fm[:], T.fm[:], T.mm[:], A.add)
        V(tt, "cb ci", "cb", T.cb[:], T.cb[:], T.ci[:], A.add)
        for l in (4, 0): V(cp, "fm", "o%d" % l, T["o%d" % l][:], T.fm[:, :, l])
        S("rw5 rw5b o4", "rw4", T.rw4[:, 0:C], pick("rw5", 0, 768, "o4"))
        S("rw4", "rw4b", T.rw4[:, C:768], T.rw4[:, 0:C], F.Identity, bias=768.0)
        if r == 0:
            sp_table(0)
            t2_table(0, "s", 2, 2)
        V(cp, "sw sw1 o1", "a1", T.a1[:], pick("sw", 0, 768, "o1"))
        V(cp, "fm", "o3", T.o3[:], T.fm[:, :, 3])
        S("rw4 rw4b o3", "rw3", T.rw3[:, 0:C], pick("rw4", 0, 768, "o3"))
        S("rw3", "rw3b", T.rw3[:, C:768], T.rw3[:, 0:C], F.Identity, bias=384.0)
        take("a1", "a1 o0", "o0", "mk", "am")
        V(cp, "fm", "o2", T.o2[:], T.fm[:, :, 2])
        gather_sum("am", "an", "r16")
        S("rw3 rw3b o2", "rw2", T.rw2[:], pick("rw3", 0, 768, "o2"), F.Identity, bias=192.0)
        V(ts, "an", "hb", T.hb[:], last("an"), 1024.0 * Q, 768.0, A.is_ge, A.mult)
        V(ts, "an", "ya", T.ya[:], last("an"), 1 / Q, None, A.mult)
        V(tt, "hb cb", "hb", T.hb[:], T.hb[:], T.cb[:], A.add)
        V(ts, "ya", "ya", T.ya[:], T.ya[:], 511, None, A.bitwise_and)
        V(cp, "hb", "oa", T.oa[:], T.hb[:])
        V(cp, "ya", "oi", T.oi[:], T.ya[:])
        if r == 0:
            V(ts, "ib", "ib", T.ib[:], T.ib[:], 15, None, A.bitwise_and)
            t2_table(0, "v", 0, 2)
        for c in range(2): half(r, c)
        T2 = "t2.0 t2.1 t2.2 t2.3"

        def first_two():
            take("t2", T2 + " oa", "oa", "mk", "km", 0, 1536)
            gather_sum("km", "ks", "r16")

        def own_ends(t): V(ts, "yi", "oi6.%d" % t, T.oi6[:, 24 * t:24 * t + 24], T.yi[:], 4.0, float(t), A.mult, A.add)
        first_two()
        if r == 0:
            V(ts, "ib", "mk4", T.mk4[:], T.ib[:], 3.0, None, A.is_le)
            V(ts, "ic", "ic", T.ic[:], T.ic[:], 15, None, A.bitwise_and)
        take("rw2", "rw2 oi", "oi", "mk", "am")
        gather_sum("am", "an", "r16")
        V(ts, "an", "yb", T.yb[:], last("an"), 1 / Q, None, A.mult)
        V(tt, "an ks", "fk", T.fk[:], last("an"), last("ks"), A.add)
        V(ts, "yb", "yi", T.yi[:], T.yb[:], 511, None, A.bitwise_and)
        V(ts, "yb", "yw", T.yw[:], T.yb[:], 1536, None, A.bitwise_and)
        V(cp, "fk", "ob", T.ob[:], T.fk[:])
        for t in (0, 1): own_ends(t)
        take("t2", T2 + " ob", "ob", "mk", "km", 0, 1536)
        for t in (2, 3): own_ends(t)
        for c, (a, b) in enumerate(CH):
            for t in range(4):
                S("%s.0 %s.1 oi6.%d" % (X, X, t), "xi.%d.%d" % (c, t), T.xi[:, 4 * a + t:4 * b:4],
                  pick(X, 0, 4 * C, "oi6", 24 * t + a // 16, 24 * t + b // 16), F.Copy, scale=0.5)
        V(ts, "yw", "w4", T.w4[:], T.yw[:], 0.75, 192.0, A.mult, A.add)
        gather_sum("km", "ks", "r16")
        V(tt, "ks w4", "w4", T.w4[:], last("ks"), T.w4[:], A.add)
        V(cp, "w4", "oc6", T.oc6[:], T.w4[:])
        take("t2", T2 + " oc6", "oc6", "mk4", "km", 0, 1536)
        gather_sum("km", "ks", "r4")
        V(ts, "ks pq", "oz", T.oz[:], last("ks", 0, 4), 4.0, T.pq[:, 0:1], A.mult, A.add)
        def layer(z, k, q):
            o, W, B = T.ht[:, 512 * z + k:512 * z + 512:4], "ht.%d.%d" % (z, k), 4 * (z % 2) + k
            if q == "s": S("B%d" % B, W, o, bank(B, 128), F.Copy, scale=0.03125)
            else: V(ts, "B%d" % B, W, o, bank(B, 128), 0.03125, None, A.mult)

        for z in range(3):
            a = 128 * z
            V(tt, "xh.0 xh.1 oz " + " ".join("xi.%d.%d" % (z // 2, t) for t in range(4)), "zt.%d" % z, T.zt[:, 4 * a:4 * a + 512],
              pick("xh", 0, 4 * C, "oz", a // 4, a // 4 + 32), T.xi[:, 4 * a:4 * a + 512], A.add)
            V(qz, "zt.%d" % z, "z.%d" % z, T.zq[:, a:a + 128], T.zs[:, a:a + 128], T.zt[:, 4 * a:4 * a + 512])
            for k in range(4): mm(4 * (z % 2) + k, 128, "layq lays z.%d" % z, "lay", 128 * k, "z", a)
            if z < 2:
                for k in range(4): layer(z, k, "s")
        if r == 0:
            V(ts, "ic", "mkc", T.mkc[:], T.ic[:], 1.0, None, A.is_le)

        def ship(c):
            a, b = CH[c]
            h, l = "h%d" % r, "l%d" % r
            V(qz, " ".join("ht.%d.%d" % (z, k) for z in range(a // 128, b // 128) for k in range(4)), "%s.%d" % (h, c),
              T[h + "q"][:, a:b], T[h + "s"][:, a:b], T.ht[:, 4 * a:4 * b])
            send(dst, "%s.%d" % (h, c), "h%d_%d" % (r, c), [(T[l + "q"][:, a:b].bitcast(dt.uint8), T[h + "q"][:, a:b].bitcast(dt.uint8)),
                                                         (T[l + "s"][:, a:b], T[h + "s"][:, a:b])])
        ship(0)
        take("t2", T2 + " oc6", "oc6", "mk", "km", 0, 1536)
        mm(4, C, "p6 p6s xq.0 xq.1", "p6", 0, "x", 0)
        for k in range(4): layer(2, k, "s")
        S("B4", "e6", T.e6[:], bank(4, C), F.Sign, bias=-(2.0 ** -93))
        gather_sum("km", "ks", "r16")
        ship(1)
        V(ts, "ks", "oe", T.oe[:], last("ks"), 192.0, None, A.add)
        take("e6", "e6 oe", "oe", "mkc", "km")
        gather_sum("km", "ks", "r16")
        V(ts, "ks pd", "fe", T.fe[:], last("ks"), 0.0, T.pd[:, 0:1], A.is_equal, A.mult)
        V(tt, "fe ci", "fe", T.fe[:], T.fe[:], T.ci[:], A.add)
        V(cp, "fe", "ot", T.ot[:], T.fe[:])
        S("sp ot", "yy", T.yy[:, 0:C], pick("sp", 0, C, "ot"))
        V(cp, "sp ot", "yy1", T.yy[:, C:768], pick("sp", C, 768, "ot"))
        L, N = "ls%d" % r, "ls%d" % (r + 1)
        if r < 2:
            V(tt, "yy1 %s mk" % L, "tm", T.tm[:, 0:C], pick("yy", C, 768, L), T.mk[:], A.mult)
            V(tt, "yy %sb mk" % L, "tm1", T.tm[:, C:768], pick("yy", 0, C, L, 24, 48), T.mk[:], A.mult)
            V(scan, "tm tm1 r16", "tn", T.tn[:], T.r16[:], T.tm[:], 0.0, A.mult, A.add)
            V(ts, "tn", N + " " + N + "b", T[N][:], T.tn[:, 15:768:16], 192.0, None, A.add)
            send_lists(r + 1)
            S("yy %sb" % L, "sw", T.sw[:, 0:C], pick("yy", 0, C, L, 24, 48), F.Identity, scale=Q, bias=192.0 * Q)
            S("yy1 %s" % L, "sw1", T.sw[:, C:768], pick("yy", C, 768, L), F.Identity, scale=Q, bias=1216.0 * Q)
        V(tt, "yy %sb mk4" % L, "km", T.km[:], pick("yy", 0, C, L, 24, 48), T.mk4[:], A.mult)
        gather_sum("km", "ks", "r4")
        V(ts, "ks pq", "od", T.od[:], last("ks", 0, 4), 4.0, T.pq[:, 0:1], A.mult, A.add)
        if r == 0:
            for k in range(4): V(qz, "et%d" % k, "e%d" % k, T["e%dq" % k][:], T["e%ds" % k][:], T["et%d" % k][:])
            V(qz, "vt", "pv", T.pvq[:], T.pvs[:], T.vt[:])
        if r < 2: prepare("tn", T.tn[:, 15:C:16], T.tn[:, C + 15:768:16], 192.0)
        for c, (a, b) in enumerate(CH):
            for k in range(4): mm(4 * c + k, b - a, "e%d l%d.%d" % (k, r, c), "e%d" % k, 0, "l%d" % r, a)
            for k in range(4):
                o, W, B = T.dd[:, 4 * a + k:4 * b:4], "dd.%d.%d" % (c, k), "B%d" % (4 * c + k)
                if c == 1 and k > 1: V(cp, B, W, o, bank(4 * c + k, b - a))
                else: S(B, W, o, bank(4 * c + k, b - a))
        if r < 2: sp_table(r + 1)
        else:
            S("yy %sb" % L, "sod", T.sod[:, 0:C], pick("yy", 0, C, L, 24, 48), F.Identity, bias=192.0)
            S("yy1 %s" % L, "sod1", T.sod[:, C:768], pick("yy", C, 768, L), F.Identity, bias=192.0)
            ends = [D("g", "sod sod1", "", T["so"][:], T.sod[0:128:16, :])]
        for c, (a, b) in enumerate(CH):
            V(tt, "od %s.%d " % (X, c) + " ".join("dd.%d.%d" % (i, k) for i in range(2) for k in range(4)), "x%d.%d" % (r + 1, c),
              T["x%d" % (r + 1)][:, 4 * a:4 * b], pick("dd", 0, 4 * C, "od", a // 4, b // 4), T[X][:, 4 * a:4 * b], A.add)
            pack_state(r + 1, c)
            if r < 2:
                if c == 0: t2_table(r + 1, "s", 0, 2)
                signs(c)
            else:
                mm(c, b - a, "pv xq.%d" % c, "pv", 0, "x", a)
                if c == 0: S("B0", "yd.0", T.yd[:, a:b], bank(0, b - a))
                else: V(cp, "B1", "yd.1", T.yd[:, a:b], bank(1, b - a))
                ends.append(D("y", "xq.%d" % c, "", T.oc[:, 4 * a:4 * b], T.xq[:, a:b].bitcast(dt.uint8)))
                if c == 1:
                    for k in range(4):
                        ends.append(D("ssyg"[k], "xq.0 xq.1", "", T.osc[4 * k:4 * k + 4, 0:C], T.xs[32 * k:32 * k + 4, 0:C]))
                ends.append(D("y", "yd.%d" % c, "", T.y[:, a:b], T.yd[:, a:b]))
        if r < 2:
            t2_table(r + 1, "v", 3, 1)
            t2_table(r + 1, "s", 2, 1)
            turned(0)
            turned(1)

    for s in ends: wait("y", s, 16)
    for s in ("v", "s", "t", "i", "loc"): wait("g", s, count[s])
